import numpy as np
import ml_dtypes


def mxq(x, axis, fmt="e4m3"):
    dtype, down = {"e4m3": (ml_dtypes.float8_e4m3fn, 7), "e5m2": (ml_dtypes.float8_e5m2, 14)}[fmt]
    v = np.moveaxis(np.asarray(x, np.float32).astype(ml_dtypes.bfloat16).astype(np.float64), axis, -1)
    blocks = v.reshape(v.shape[:-1] + (-1, 32))
    amax = np.abs(blocks).max(-1, keepdims=True)
    byte = np.maximum(np.where(amax > 0, np.frexp(amax)[1] - 1 + 127, 0) - down, 1)
    scale = np.exp2(byte - 127.0)
    codes = (blocks / scale).astype(np.float32).astype(dtype).astype(np.float64)
    return np.moveaxis((codes * scale).reshape(v.shape), -1, axis)


WIDE = False


def mx_kscale(k, group=512):
    if not WIDE:
        return np.ones(k)
    levels = np.array([10, -10, 5, -5, 0])
    if group != 512:
        return np.exp2(np.random.permutation(np.resize(levels, k // group))).repeat(group)
    if k % 512:
        return np.exp2(np.random.permutation(np.resize(levels, k // 32))).repeat(32)
    a = np.empty((k // 512, 16))
    for p in range(k // 512):
        a[p, :8] = np.random.permutation(np.resize(levels, 8))
        for g in range(8):
            far = levels[np.abs(levels - a[p, g]) >= 10]
            a[p, g + 8] = far[np.random.randint(len(far))]
    return np.exp2(a.ravel()).repeat(32)


def f64(x):
    return np.asarray(x).astype(np.float64)


E2M1 = np.array([0.0, 0.5, 1.0, 1.5, 2.0, 3.0, 4.0, 6.0, -0.0, -0.5, -1.0, -1.5, -2.0, -3.0, -4.0, -6.0])


def pack_group(w):
    k, n = w.shape
    w = f64(np.asarray(w, np.float32).astype(ml_dtypes.bfloat16)).reshape(k // 32, 32, n)
    amax = np.abs(w).max(1)
    mant, ex = np.frexp(amax / 6.0)
    byte = np.clip(np.where(amax > 0, np.where(mant > 0.5, ex, ex - 1) + 127, 1), 1, 254)
    scaled = (w * np.exp2(127.0 - byte)[:, None, :]).reshape(k, n).astype(np.float32)
    c = np.ascontiguousarray(scaled.reshape(k // 4, 4, n).transpose(0, 2, 1)).astype(ml_dtypes.float4_e2m1fn).view(np.uint8) & 0xF
    return np.ascontiguousarray((c[..., 0::2] | (c[..., 1::2] << 4)).reshape(k // 4, 2 * n)), byte.astype(np.uint8)


def unpack_group(words, scales):
    p, n = words.shape[0], scales.shape[1]
    words = np.ascontiguousarray(words).reshape(p, n, 2)
    nib = np.empty((p, n, 4), np.uint8)
    nib[..., 0::2] = words & 0xF
    nib[..., 1::2] = words >> 4
    return E2M1[nib].transpose(0, 2, 1).reshape(4 * p, n) * np.repeat(np.exp2(scales.astype(np.float64) - 127.0), 32, axis=0)


def silu(v):
    return v / (1.0 + np.exp(-v))


G, D, M, O, N = 2, 256, 256, 256, 512


def setup_inputs():
    n = np.random.standard_normal
    s_d = mx_kscale(D, 0)
    s_o = mx_kscale(O, 0)
    w1_ = [pack_group(w) for w in n((G, D, M)) / np.sqrt(D) / s_d[:, None]]
    w2_ = [pack_group(w) for w in n((G, D, M)) / np.sqrt(D) / s_d[:, None]]
    wo_ = [pack_group(w) for w in n((G, O, M)) / np.sqrt(O) / s_o[:, None]]
    return {
        "x": (n((G, D, N)) * s_d[:, None]).astype(np.float32),
        "w1_words": np.stack([w[0] for w in w1_]),
        "w1_scales": np.stack([w[1] for w in w1_]),
        "w2_words": np.stack([w[0] for w in w2_]),
        "w2_scales": np.stack([w[1] for w in w2_]),
        "sh": (np.random.uniform(0.1, 0.4, (G, M, 1))).astype(np.float32),
        "d0": (np.random.uniform(5.0, 9.0, (G, M, N))).astype(np.float32),
        "wo_words": np.stack([w[0] for w in wo_]),
        "wo_scales": np.stack([w[1] for w in wo_]),
        "dy": (n((G, O, N)) * s_o[:, None]).astype(np.float32),
        "old": (0.03 * n((G, M, N))).astype(np.float32),
    }


def reference(x, w1_words, w1_scales, w2_words, w2_scales, sh, d0, wo_words, wo_scales, dy, old):
    w1 = np.stack([unpack_group(w1_words[g], w1_scales[g]) for g in range(G)])
    xq = mxq(f64(x), 1, "e4m3")
    z1 = w1.transpose(0, 2, 1) @ xq
    w2 = np.stack([unpack_group(w2_words[g], w2_scales[g]) for g in range(G)])
    z2 = w2.transpose(0, 2, 1) @ xq
    q1 = f64(d0) - z1
    wo = np.stack([unpack_group(wo_words[g], wo_scales[g]) for g in range(G)])
    dyq = mxq(f64(dy), 1, "e4m3")
    c0 = wo.transpose(0, 2, 1) @ dyq
    dq1 = c0 * silu(z2) / np.square(q1 * f64(sh) + 1.0) * (-1.0) * f64(sh)
    dz1 = dq1 * (-1.0)
    y = dz1 + f64(old)
    return y

@@ -1,0 +1,175 @@
+from contextlib import ExitStack
+
+import concourse.mybir as mybir
+
+G, D, M, N = 2, 256, 256, 512
+FLOPS = 3 * 2 * G * D * M * N
+
+F32 = mybir.dt.float32
+BF16 = mybir.dt.bfloat16
+I32 = mybir.dt.int32
+U32 = mybir.dt.uint32
+U8 = mybir.dt.uint8
+FP8X4 = mybir.dt.float8_e4m3fn_x4
+FP4X4 = mybir.dt.float4_e2m1fn_x4
+ACT = mybir.ActivationFunctionType
+ALU = mybir.AluOpType
+
+P = 128
+PACK = 4
+ROWS = D // PACK
+HALVES = M // P
+CHUNKS = [(0, 256), (256, 512)]
+TILES = [(g, h) for h in range(HALVES) for g in range(G)]
+
+
+def tile_rows_bkernstudent_kernel(tc, x, w1_words, w1_scales, w2_words, w2_scales, sh, d0,
+                                      wo_words, wo_scales, dy, old, out):
+    nc = tc.nc
+    with ExitStack() as ctx:
+        sb = ctx.enter_context(tc.tile_pool(name="sb", bufs=1))
+        ps = ctx.enter_context(tc.psum_pool(name="ps", bufs=1))
+        ctx.enter_context(tc.manual_schedule())
+
+        def load_words(queue, words, name):
+            t = sb.tile([P, 2 * M], U8, name=name, align_bytes=64)
+            queue.dma_start(out=t[:].bitcast(I32), in_=words.rearrange("g p b -> (g p) b").bitcast(I32))
+            return t
+
+        def load_scales(queue, scales, plane, q):
+            rows = scales.rearrange("g t m -> (g t) m").bitcast(I32)
+            queue.dma_start(out=plane[32 * q:32 * q + 4, :].bitcast(I32), in_=rows[4 * q:4 * q + 4, :])
+
+        def load_chunk(src, c, name):
+            a, b = CHUNKS[c]
+            t = sb.tile([P, PACK, b - a], F32, name=name, align_bytes=64)
+            nc.sync.dma_start(out=t[:], in_=src.rearrange("g (p j) n -> (g p) j n", j=PACK)[:, :, a:b])
+            return t
+
+        def load_half(src, h, name):
+            t = sb.tile([P, G, N], F32, name=name, align_bytes=64)
+            nc.sync.dma_start(out=t[:], in_=src[:, h * P:(h + 1) * P, :].rearrange("g p n -> p g n"))
+            return t
+
+        def interleave(raw, name):
+            width = raw.shape[2]
+            t = sb.tile([P, width, PACK], BF16, name=name, align_bytes=64)
+            nc.vector.tensor_copy(out=t[:].rearrange("p (c i) j -> p c j i", i=4),
+                                  in_=raw[:].rearrange("p j (c i) -> p c j i", i=4))
+            return t
+
+        def quantize(grouped, c, codes, scales):
+            a, b = CHUNKS[c]
+            nc.vector.quantize_mx(out=codes[:, a:b].bitcast(FP8X4), scales=scales[:, a:b],
+                                  in_=grouped[:].rearrange("p n j -> p (n j)"))
+
+        def product(bank, i, words, plane, codes, scales):
+            g, h = TILES[i]
+            r = slice(ROWS * g, ROWS * (g + 1))
+            nc.tensor.matmul_mx(out=bank[:], lhsT=words[r, 2 * P * h:2 * P * (h + 1)].bitcast(FP4X4),
+                                lhsT_scale=plane[r, P * h:P * (h + 1)],
+                                rhs=codes[r, :].bitcast(FP8X4), rhs_scale=scales[r, :],
+                                start=True, stop=True)
+
+        w2_plane = sb.tile([P, M], U8, align_bytes=64)
+        wo_plane = sb.tile([P, M], U8, align_bytes=64)
+        w1_plane = sb.tile([P, M], U8, align_bytes=64)
+        nc.vector.memset(w2_plane[:].bitcast(U32), 0)
+        nc.vector.memset(wo_plane[:].bitcast(U32), 0)
+        nc.gpsimd.memset(w1_plane[:].bitcast(U32), 0)
+
+        for q in range(4):
+            load_scales(nc.gpsimd, w1_scales, w1_plane, q)
+        x_raw = [load_chunk(x, 0, "x_raw0")]
+        load_scales(nc.scalar, w2_scales, w2_plane, 0)
+        x_raw.append(load_chunk(x, 1, "x_raw1"))
+        load_scales(nc.scalar, w2_scales, w2_plane, 1)
+        w2_sb = load_words(nc.sync, w2_words, "w2_sb")
+        load_scales(nc.scalar, w2_scales, w2_plane, 2)
+        dy_raw = [load_chunk(dy, 0, "dy_raw0")]
+        load_scales(nc.scalar, w2_scales, w2_plane, 3)
+        dy_raw.append(load_chunk(dy, 1, "dy_raw1"))
+        load_scales(nc.scalar, wo_scales, wo_plane, 0)
+        w1_sb = load_words(nc.sync, w1_words, "w1_sb")
+        load_scales(nc.scalar, wo_scales, wo_plane, 1)
+        d0_half = [load_half(d0, 0, "d0_half0")]
+        load_scales(nc.scalar, wo_scales, wo_plane, 2)
+        wo_sb = load_words(nc.sync, wo_words, "wo_sb")
+        load_scales(nc.scalar, wo_scales, wo_plane, 3)
+        sh_sb = sb.tile([P, G * HALVES], F32, align_bytes=64)
+        with nc.allow_non_contiguous_dma(reason="one sharpness value a partition"):
+            nc.sync.dma_start(out=sh_sb[:], in_=sh.rearrange("g (h p) o -> p (g h o)", p=P))
+        d0_half.append(load_half(d0, 1, "d0_half1"))
+        old_half = [load_half(old, h, "old_half%d" % h) for h in range(HALVES)]
+        d0_sb = [d0_half[h][:, g, :] for g, h in TILES]
+        old_sb = [old_half[h][:, g, :] for g, h in TILES]
+
+        def sharp(i):
+            g, h = TILES[i]
+            k = g * HALVES + h
+            return sh_sb[:, k:k + 1]
+
+        x_codes = sb.tile([P, N], U32, align_bytes=64)
+        x_scales = sb.tile([P, N], U8, align_bytes=64)
+        dy_codes = sb.tile([P, N], U32, align_bytes=64)
+        dy_scales = sb.tile([P, N], U8, align_bytes=64)
+        for c in range(len(CHUNKS)):
+            quantize(interleave(x_raw[c], "x_bf%d" % c), c, x_codes, x_scales)
+
+        gate_bank = [ps.tile([P, N], F32, name="gate_bank%d" % i) for i in range(4)]
+        z1_bank = [ps.tile([P, N], F32, name="z1_bank%d" % i) for i in range(4)]
+        work = lambda name: [sb.tile([P, N], F32, name="%s%d" % (name, i), align_bytes=64) for i in range(4)]
+        gate, dist, root, inv, inv2, grad, prod, res = [work(s) for s in
+            ("gate", "dist", "root", "inv", "inv2", "grad", "prod", "res")]
+
+        for i in range(4):
+            product(gate_bank[i], i, w2_sb, w2_plane, x_codes, x_scales)
+        for i in range(4):
+            product(z1_bank[i], i, w1_sb, w1_plane, x_codes, x_scales)
+        for i in range(4):
+            nc.scalar.activation(out=gate[i][:], in_=gate_bank[i][:], func=ACT.Silu)
+
+        for c in range(len(CHUNKS)):
+            quantize(interleave(dy_raw[c], "dy_bf%d" % c), c, dy_codes, dy_scales)
+        for i in range(4):
+            product(gate_bank[i], i, wo_sb, wo_plane, dy_codes, dy_scales)
+
+        def distance(i):
+            nc.vector.tensor_tensor(out=dist[i][:], in0=d0_sb[i], in1=z1_bank[i][:], op=ALU.subtract)
+
+        def gated(i):
+            nc.vector.tensor_tensor(out=grad[i][:], in0=gate_bank[i][:], in1=gate[i][:], op=ALU.mult)
+
+        def rsqrt(i):
+            nc.scalar.activation(out=root[i][:], in_=dist[i][:], func=ACT.Abs_reciprocal_sqrt,
+                                 scale=sharp(i), bias=1.0)
+
+        def sq1(i):
+            nc.scalar.activation(out=inv[i][:], in_=root[i][:], func=ACT.Square)
+
+        def sq2(i):
+            nc.scalar.activation(out=inv2[i][:], in_=inv[i][:], func=ACT.Square)
+
+        def scaled(i):
+            nc.vector.scalar_tensor_tensor(out=prod[i][:], in0=grad[i][:], scalar=sharp(i), in1=inv2[i][:],
+                                           op0=ALU.mult, op1=ALU.mult)
+
+        def finish(i):
+            g, h = TILES[i]
+            nc.vector.tensor_tensor(out=res[i][:], in0=prod[i][:], in1=old_sb[i], op=ALU.add)
+            nc.sync.dma_start(out=out[g, h * P:(h + 1) * P, :], in_=res[i][:])
+
+        for pair in ((0, 1), (2, 3)):
+            for stage in (distance, gated):
+                for i in pair:
+                    stage(i)
+        for step in range(4 + 2):
+            if step < 4:
+                rsqrt(step)
+            if 1 <= step < 5:
+                sq1(step - 1)
+            if 2 <= step:
+                sq2(step - 2)
+        for i in range(4):
+            scaled(i)
+            finish(i)

@@ -40,10 +40,9 @@ def tile_rows_bkernstudent_kernel(tc, x, w1_words, w1_scales, w2_words, w2_scale
             rows = scales.rearrange("g t m -> (g t) m").bitcast(I32)
             queue.dma_start(out=plane[32 * q:32 * q + 4, :].bitcast(I32), in_=rows[4 * q:4 * q + 4, :])
 
-        def load_chunk(src, c, name):
-            a, b = CHUNKS[c]
-            t = sb.tile([P, PACK, b - a], F32, name=name, align_bytes=64)
-            nc.sync.dma_start(out=t[:], in_=src.rearrange("g (p j) n -> (g p) j n", j=PACK)[:, :, a:b])
+        def load_chunk(src, u, name):
+            t = sb.tile([P, 2, N], F32, name=name, align_bytes=64)
+            nc.sync.dma_start(out=t[:], in_=src.rearrange("g (p j) n -> (g p) j n", j=PACK)[:, 2 * u:2 * u + 2, :])
             return t
 
         def load_half(src, h, name):
@@ -51,17 +50,13 @@ def tile_rows_bkernstudent_kernel(tc, x, w1_words, w1_scales, w2_words, w2_scale
             nc.sync.dma_start(out=t[:], in_=src[:, h * P:(h + 1) * P, :].rearrange("g p n -> p g n"))
             return t
 
-        def interleave(raw, name):
-            width = raw.shape[2]
-            t = sb.tile([P, width, PACK], BF16, name=name, align_bytes=64)
-            nc.vector.tensor_copy(out=t[:].rearrange("p (c i) j -> p c j i", i=4),
-                                  in_=raw[:].rearrange("p j (c i) -> p c j i", i=4))
-            return t
+        def interleave(copy, raw, u, grouped, a, b):
+            copy(out=grouped[:, a:b, 2 * u:2 * u + 2], in_=raw[:, :, a:b].rearrange("p j n -> p n j"))
 
         def quantize(grouped, c, codes, scales):
             a, b = CHUNKS[c]
             nc.vector.quantize_mx(out=codes[:, a:b].bitcast(FP8X4), scales=scales[:, a:b],
-                                  in_=grouped[:].rearrange("p n j -> p (n j)"))
+                                  in_=grouped[:, a:b, :].rearrange("p n j -> p (n j)"))
 
         def product(bank, i, words, plane, codes, scales):
             g, h = TILES[i]
@@ -74,10 +69,14 @@ def tile_rows_bkernstudent_kernel(tc, x, w1_words, w1_scales, w2_words, w2_scale
         w2_plane = sb.tile([P, M], U8, align_bytes=64)
         wo_plane = sb.tile([P, M], U8, align_bytes=64)
         w1_plane = sb.tile([P, M], U8, align_bytes=64)
+        sh_rows = sb.tile([P, P], F32, align_bytes=64)
         nc.vector.memset(w2_plane[:].bitcast(U32), 0)
         nc.vector.memset(wo_plane[:].bitcast(U32), 0)
+        nc.gpsimd.memset(sh_rows[:], 0.0)
         nc.gpsimd.memset(w1_plane[:].bitcast(U32), 0)
 
+        nc.gpsimd.dma_start(out=sh_rows[0:P:32, :].rearrange("q (c b) -> q c b", b=32),
+                            in_=sh.rearrange("g (h q b) o -> q (g h) (b o)", q=4, b=32))
         for q in range(4):
             load_scales(nc.gpsimd, w1_scales, w1_plane, q)
         x_raw = [load_chunk(x, 0, "x_raw0")]
@@ -89,32 +88,39 @@ def tile_rows_bkernstudent_kernel(tc, x, w1_words, w1_scales, w2_words, w2_scale
         dy_raw = [load_chunk(dy, 0, "dy_raw0")]
         load_scales(nc.scalar, w2_scales, w2_plane, 3)
         dy_raw.append(load_chunk(dy, 1, "dy_raw1"))
-        load_scales(nc.scalar, wo_scales, wo_plane, 0)
         w1_sb = load_words(nc.sync, w1_words, "w1_sb")
-        load_scales(nc.scalar, wo_scales, wo_plane, 1)
-        d0_half = [load_half(d0, 0, "d0_half0")]
-        load_scales(nc.scalar, wo_scales, wo_plane, 2)
         wo_sb = load_words(nc.sync, wo_words, "wo_sb")
-        load_scales(nc.scalar, wo_scales, wo_plane, 3)
-        sh_sb = sb.tile([P, G * HALVES], F32, align_bytes=64)
-        with nc.allow_non_contiguous_dma(reason="one sharpness value a partition"):
-            nc.sync.dma_start(out=sh_sb[:], in_=sh.rearrange("g (h p) o -> p (g h o)", p=P))
+        d0_half = [load_half(d0, 0, "d0_half0")]
+        for q in range(4):
+            load_scales(nc.sync, wo_scales, wo_plane, q)
         d0_half.append(load_half(d0, 1, "d0_half1"))
         old_half = [load_half(old, h, "old_half%d" % h) for h in range(HALVES)]
         d0_sb = [d0_half[h][:, g, :] for g, h in TILES]
         old_sb = [old_half[h][:, g, :] for g, h in TILES]
 
+        warm = sb.tile([P, 2], F32, align_bytes=64)
+        nc.vector.memset(warm[:, 0:1], 0.0)
+        nc.scalar.activation(out=warm[:, 1:2], in_=warm[:, 0:1], func=ACT.Silu)
+
+        sh_sb = sb.tile([P, P], F32, align_bytes=64)
+
         def sharp(i):
             g, h = TILES[i]
-            k = g * HALVES + h
+            k = 32 * (g * HALVES + h)
             return sh_sb[:, k:k + 1]
 
         x_codes = sb.tile([P, N], U32, align_bytes=64)
         x_scales = sb.tile([P, N], U8, align_bytes=64)
         dy_codes = sb.tile([P, N], U32, align_bytes=64)
         dy_scales = sb.tile([P, N], U8, align_bytes=64)
-        for c in range(len(CHUNKS)):
-            quantize(interleave(x_raw[c], "x_bf%d" % c), c, x_codes, x_scales)
+        x_bf = sb.tile([P, N, PACK], BF16, align_bytes=64)
+        dy_bf = sb.tile([P, N, PACK], BF16, align_bytes=64)
+        for u in range(2):
+            interleave(nc.vector.tensor_copy, x_raw[u], u, x_bf, 0, N // 2)
+            interleave(nc.vector.tensor_copy, x_raw[u], u, x_bf, N // 2, 352)
+            interleave(nc.scalar.copy, x_raw[u], u, x_bf, 352, N)
+        for c in range(2):
+            quantize(x_bf, c, x_codes, x_scales)
 
         gate_bank = [ps.tile([P, N], F32, name="gate_bank%d" % i) for i in range(4)]
         z1_bank = [ps.tile([P, N], F32, name="z1_bank%d" % i) for i in range(4)]
@@ -125,51 +131,49 @@ def tile_rows_bkernstudent_kernel(tc, x, w1_words, w1_scales, w2_words, w2_scale
         for i in range(4):
             product(gate_bank[i], i, w2_sb, w2_plane, x_codes, x_scales)
         for i in range(4):
-            product(z1_bank[i], i, w1_sb, w1_plane, x_codes, x_scales)
-        for i in range(4):
             nc.scalar.activation(out=gate[i][:], in_=gate_bank[i][:], func=ACT.Silu)
 
-        for c in range(len(CHUNKS)):
-            quantize(interleave(dy_raw[c], "dy_bf%d" % c), c, dy_codes, dy_scales)
-        for i in range(4):
-            product(gate_bank[i], i, wo_sb, wo_plane, dy_codes, dy_scales)
-
-        def distance(i):
-            nc.vector.tensor_tensor(out=dist[i][:], in0=d0_sb[i], in1=z1_bank[i][:], op=ALU.subtract)
-
-        def gated(i):
-            nc.vector.tensor_tensor(out=grad[i][:], in0=gate_bank[i][:], in1=gate[i][:], op=ALU.mult)
-
-        def rsqrt(i):
-            nc.scalar.activation(out=root[i][:], in_=dist[i][:], func=ACT.Abs_reciprocal_sqrt,
-                                 scale=sharp(i), bias=1.0)
-
-        def sq1(i):
-            nc.scalar.activation(out=inv[i][:], in_=root[i][:], func=ACT.Square)
-
-        def sq2(i):
-            nc.scalar.activation(out=inv2[i][:], in_=inv[i][:], func=ACT.Square)
-
-        def scaled(i):
-            nc.vector.scalar_tensor_tensor(out=prod[i][:], in0=grad[i][:], scalar=sharp(i), in1=inv2[i][:],
-                                           op0=ALU.mult, op1=ALU.mult)
-
-        def finish(i):
-            g, h = TILES[i]
-            nc.vector.tensor_tensor(out=res[i][:], in0=prod[i][:], in1=old_sb[i], op=ALU.add)
-            nc.sync.dma_start(out=out[g, h * P:(h + 1) * P, :], in_=res[i][:])
+        interleave(nc.vector.tensor_copy, dy_raw[0], 0, dy_bf, 0, N)
+        nc.vector.transpose(out=sh_sb[:], in_=sh_rows[:])
+        for a, b in CHUNKS:
+            interleave(nc.vector.tensor_copy, dy_raw[1], 1, dy_bf, a, b)
+        for c in range(2):
+            quantize(dy_bf, c, dy_codes, dy_scales)
 
         for pair in ((0, 1), (2, 3)):
-            for stage in (distance, gated):
-                for i in pair:
-                    stage(i)
-        for step in range(4 + 2):
-            if step < 4:
-                rsqrt(step)
-            if 1 <= step < 5:
-                sq1(step - 1)
-            if 2 <= step:
-                sq2(step - 2)
+            for i in pair:
+                product(z1_bank[i], i, w1_sb, w1_plane, x_codes, x_scales)
+            for i in pair:
+                product(gate_bank[i], i, wo_sb, wo_plane, dy_codes, dy_scales)
+            for i in pair:
+                nc.vector.tensor_tensor(out=dist[i][:], in0=d0_sb[i], in1=z1_bank[i][:], op=ALU.subtract)
+            for i in pair:
+                nc.vector.tensor_tensor(out=grad[i][:], in0=gate_bank[i][:], in1=gate[i][:], op=ALU.mult)
+
+        parts = [slice(0, N // 2), slice(N // 2, N)]
         for i in range(4):
-            scaled(i)
-            finish(i)
+            g, h = TILES[i]
+            twice = i in (2,)
+            for c in parts:
+                nc.scalar.activation(out=root[i][:, c], in_=dist[i][:, c], func=ACT.Abs_reciprocal_sqrt,
+                                     scale=sharp(i), bias=1.0)
+            for c in parts:
+                nc.scalar.activation(out=inv[i][:, c], in_=root[i][:, c], func=ACT.Square)
+            if twice:
+                for c in parts:
+                    nc.vector.tensor_tensor(out=inv2[i][:, c], in0=grad[i][:, c], in1=inv[i][:, c], op=ALU.mult)
+                for c in parts:
+                    nc.vector.scalar_tensor_tensor(out=prod[i][:, c], in0=inv2[i][:, c], scalar=sharp(i),
+                                                   in1=inv[i][:, c], op0=ALU.mult, op1=ALU.mult)
+            else:
+                for c in parts:
+                    nc.scalar.activation(out=inv2[i][:, c], in_=inv[i][:, c], func=ACT.Square)
+                for c in parts:
+                    nc.vector.scalar_tensor_tensor(out=prod[i][:, c], in0=grad[i][:, c], scalar=sharp(i),
+                                                   in1=inv2[i][:, c], op0=ALU.mult, op1=ALU.mult)
+            for c in parts:
+                nc.vector.tensor_tensor(out=res[i][:, c], in0=prod[i][:, c], in1=old_sb[i][:, c], op=ALU.add)
+                if i == 3:
+                    nc.sync.dma_start(out=out[g, h * P:(h + 1) * P, c], in_=res[i][:, c])
+            if i < 3:
+                nc.sync.dma_start(out=out[g, h * P:(h + 1) * P, :], in_=res[i][:])

from contextlib import ExitStack

import concourse.mybir as mybir

G, D, M, N = 2, 256, 256, 512
FLOPS = 3 * 2 * G * D * M * N

F32 = mybir.dt.float32
BF16 = mybir.dt.bfloat16
I32 = mybir.dt.int32
U32 = mybir.dt.uint32
U8 = mybir.dt.uint8
FP8X4 = mybir.dt.float8_e4m3fn_x4
FP4X4 = mybir.dt.float4_e2m1fn_x4
ACT = mybir.ActivationFunctionType
ALU = mybir.AluOpType

P = 128
PACK = 4
ROWS = D // PACK
HALVES = M // P
CHUNKS = [(0, 256), (256, 512)]
TILES = [(g, h) for h in range(HALVES) for g in range(G)]


def tile_rows_bkernstudent_kernel(tc, x, w1_words, w1_scales, w2_words, w2_scales, sh, d0,
                                      wo_words, wo_scales, dy, old, out):
    nc = tc.nc
    with ExitStack() as ctx:
        sb = ctx.enter_context(tc.tile_pool(name="sb", bufs=1))
        ps = ctx.enter_context(tc.psum_pool(name="ps", bufs=1))
        ctx.enter_context(tc.manual_schedule())

        def load_words(queue, words, name):
            t = sb.tile([P, 2 * M], U8, name=name, align_bytes=64)
            queue.dma_start(out=t[:].bitcast(I32), in_=words.rearrange("g p b -> (g p) b").bitcast(I32))
            return t

        def load_scales(queue, scales, plane, q):
            rows = scales.rearrange("g t m -> (g t) m").bitcast(I32)
            queue.dma_start(out=plane[32 * q:32 * q + 4, :].bitcast(I32), in_=rows[4 * q:4 * q + 4, :])

        def load_chunk(src, u, name):
            t = sb.tile([P, 2, N], F32, name=name, align_bytes=64)
            nc.sync.dma_start(out=t[:], in_=src.rearrange("g (p j) n -> (g p) j n", j=PACK)[:, 2 * u:2 * u + 2, :])
            return t

        def load_half(src, h, name):
            t = sb.tile([P, G, N], F32, name=name, align_bytes=64)
            nc.sync.dma_start(out=t[:], in_=src[:, h * P:(h + 1) * P, :].rearrange("g p n -> p g n"))
            return t

        def interleave(copy, raw, u, grouped, a, b):
            copy(out=grouped[:, a:b, 2 * u:2 * u + 2], in_=raw[:, :, a:b].rearrange("p j n -> p n j"))

        def quantize(grouped, c, codes, scales):
            a, b = CHUNKS[c]
            nc.vector.quantize_mx(out=codes[:, a:b].bitcast(FP8X4), scales=scales[:, a:b],
                                  in_=grouped[:, a:b, :].rearrange("p n j -> p (n j)"))

        def product(bank, i, words, plane, codes, scales):
            g, h = TILES[i]
            r = slice(ROWS * g, ROWS * (g + 1))
            nc.tensor.matmul_mx(out=bank[:], lhsT=words[r, 2 * P * h:2 * P * (h + 1)].bitcast(FP4X4),
                                lhsT_scale=plane[r, P * h:P * (h + 1)],
                                rhs=codes[r, :].bitcast(FP8X4), rhs_scale=scales[r, :],
                                start=True, stop=True)

        w2_plane = sb.tile([P, M], U8, align_bytes=64)
        wo_plane = sb.tile([P, M], U8, align_bytes=64)
        w1_plane = sb.tile([P, M], U8, align_bytes=64)
        sh_rows = sb.tile([P, P], F32, align_bytes=64)
        nc.vector.memset(w2_plane[:].bitcast(U32), 0)
        nc.vector.memset(wo_plane[:].bitcast(U32), 0)
        nc.gpsimd.memset(sh_rows[:], 0.0)
        nc.gpsimd.memset(w1_plane[:].bitcast(U32), 0)

        nc.gpsimd.dma_start(out=sh_rows[0:P:32, :].rearrange("q (c b) -> q c b", b=32),
                            in_=sh.rearrange("g (h q b) o -> q (g h) (b o)", q=4, b=32))
        for q in range(4):
            load_scales(nc.gpsimd, w1_scales, w1_plane, q)
        x_raw = [load_chunk(x, 0, "x_raw0")]
        load_scales(nc.scalar, w2_scales, w2_plane, 0)
        x_raw.append(load_chunk(x, 1, "x_raw1"))
        load_scales(nc.scalar, w2_scales, w2_plane, 1)
        w2_sb = load_words(nc.sync, w2_words, "w2_sb")
        load_scales(nc.scalar, w2_scales, w2_plane, 2)
        dy_raw = [load_chunk(dy, 0, "dy_raw0")]
        load_scales(nc.scalar, w2_scales, w2_plane, 3)
        dy_raw.append(load_chunk(dy, 1, "dy_raw1"))
        w1_sb = load_words(nc.sync, w1_words, "w1_sb")
        wo_sb = load_words(nc.sync, wo_words, "wo_sb")
        d0_half = [load_half(d0, 0, "d0_half0")]
        for q in range(4):
            load_scales(nc.sync, wo_scales, wo_plane, q)
        d0_half.append(load_half(d0, 1, "d0_half1"))
        old_half = [load_half(old, h, "old_half%d" % h) for h in range(HALVES)]
        d0_sb = [d0_half[h][:, g, :] for g, h in TILES]
        old_sb = [old_half[h][:, g, :] for g, h in TILES]

        warm = sb.tile([P, 2], F32, align_bytes=64)
        nc.vector.memset(warm[:, 0:1], 0.0)
        nc.scalar.activation(out=warm[:, 1:2], in_=warm[:, 0:1], func=ACT.Silu)

        sh_sb = sb.tile([P, P], F32, align_bytes=64)

        def sharp(i):
            g, h = TILES[i]
            k = 32 * (g * HALVES + h)
            return sh_sb[:, k:k + 1]

        x_codes = sb.tile([P, N], U32, align_bytes=64)
        x_scales = sb.tile([P, N], U8, align_bytes=64)
        dy_codes = sb.tile([P, N], U32, align_bytes=64)
        dy_scales = sb.tile([P, N], U8, align_bytes=64)
        x_bf = sb.tile([P, N, PACK], BF16, align_bytes=64)
        dy_bf = sb.tile([P, N, PACK], BF16, align_bytes=64)
        for u in range(2):
            interleave(nc.vector.tensor_copy, x_raw[u], u, x_bf, 0, N // 2)
            interleave(nc.vector.tensor_copy, x_raw[u], u, x_bf, N // 2, 352)
            interleave(nc.scalar.copy, x_raw[u], u, x_bf, 352, N)
        for c in range(2):
            quantize(x_bf, c, x_codes, x_scales)

        gate_bank = [ps.tile([P, N], F32, name="gate_bank%d" % i) for i in range(4)]
        z1_bank = [ps.tile([P, N], F32, name="z1_bank%d" % i) for i in range(4)]
        work = lambda name: [sb.tile([P, N], F32, name="%s%d" % (name, i), align_bytes=64) for i in range(4)]
        gate, dist, root, inv, inv2, grad, prod, res = [work(s) for s in
            ("gate", "dist", "root", "inv", "inv2", "grad", "prod", "res")]

        for i in range(4):
            product(gate_bank[i], i, w2_sb, w2_plane, x_codes, x_scales)
        for i in range(4):
            nc.scalar.activation(out=gate[i][:], in_=gate_bank[i][:], func=ACT.Silu)

        interleave(nc.vector.tensor_copy, dy_raw[0], 0, dy_bf, 0, N)
        nc.vector.transpose(out=sh_sb[:], in_=sh_rows[:])
        for a, b in CHUNKS:
            interleave(nc.vector.tensor_copy, dy_raw[1], 1, dy_bf, a, b)
        for c in range(2):
            quantize(dy_bf, c, dy_codes, dy_scales)

        for pair in ((0, 1), (2, 3)):
            for i in pair:
                product(z1_bank[i], i, w1_sb, w1_plane, x_codes, x_scales)
            for i in pair:
                product(gate_bank[i], i, wo_sb, wo_plane, dy_codes, dy_scales)
            for i in pair:
                nc.vector.tensor_tensor(out=dist[i][:], in0=d0_sb[i], in1=z1_bank[i][:], op=ALU.subtract)
            for i in pair:
                nc.vector.tensor_tensor(out=grad[i][:], in0=gate_bank[i][:], in1=gate[i][:], op=ALU.mult)

        parts = [slice(0, N // 2), slice(N // 2, N)]
        for i in range(4):
            g, h = TILES[i]
            twice = i in (2,)
            for c in parts:
                nc.scalar.activation(out=root[i][:, c], in_=dist[i][:, c], func=ACT.Abs_reciprocal_sqrt,
                                     scale=sharp(i), bias=1.0)
            for c in parts:
                nc.scalar.activation(out=inv[i][:, c], in_=root[i][:, c], func=ACT.Square)
            if twice:
                for c in parts:
                    nc.vector.tensor_tensor(out=inv2[i][:, c], in0=grad[i][:, c], in1=inv[i][:, c], op=ALU.mult)
                for c in parts:
                    nc.vector.scalar_tensor_tensor(out=prod[i][:, c], in0=inv2[i][:, c], scalar=sharp(i),
                                                   in1=inv[i][:, c], op0=ALU.mult, op1=ALU.mult)
            else:
                for c in parts:
                    nc.scalar.activation(out=inv2[i][:, c], in_=inv[i][:, c], func=ACT.Square)
                for c in parts:
                    nc.vector.scalar_tensor_tensor(out=prod[i][:, c], in0=grad[i][:, c], scalar=sharp(i),
                                                   in1=inv2[i][:, c], op0=ALU.mult, op1=ALU.mult)
            for c in parts:
                nc.vector.tensor_tensor(out=res[i][:, c], in0=prod[i][:, c], in1=old_sb[i][:, c], op=ALU.add)
                if i == 3:
                    nc.sync.dma_start(out=out[g, h * P:(h + 1) * P, c], in_=res[i][:, c])
            if i < 3:
                nc.sync.dma_start(out=out[g, h * P:(h + 1) * P, :], in_=res[i][:])
